import numpy as np
import ml_dtypes


def mxq(x, axis, fmt="e4m3"):
    dtype, down = {"e4m3": (ml_dtypes.float8_e4m3fn, 7), "e5m2": (ml_dtypes.float8_e5m2, 14)}[fmt]
    v = np.moveaxis(np.asarray(x, np.float32).astype(ml_dtypes.bfloat16).astype(np.float64), axis, -1)
    blocks = v.reshape(v.shape[:-1] + (-1, 32))
    amax = np.abs(blocks).max(-1, keepdims=True)
    byte = np.maximum(np.where(amax > 0, np.frexp(amax)[1] - 1 + 127, 0) - down, 1)
    scale = np.exp2(byte - 127.0)
    codes = (blocks / scale).astype(np.float32).astype(dtype).astype(np.float64)
    return np.moveaxis((codes * scale).reshape(v.shape), -1, axis)


WIDE = False


def mx_kscale(k):
    if not WIDE:
        return np.ones(k)
    levels = np.array([10, -10, 5, -5, 0])
    if k % 512:
        return np.exp2(np.random.permutation(np.resize(levels, k // 32))).repeat(32)
    a = np.empty((k // 512, 16))
    for p in range(k // 512):
        a[p, :8] = np.random.permutation(np.resize(levels, 8))
        for g in range(8):
            far = levels[np.abs(levels - a[p, g]) >= 10]
            a[p, g + 8] = far[np.random.randint(len(far))]
    return np.exp2(a.ravel()).repeat(32)


def f64(x):
    return np.asarray(x).astype(np.float64)


def striped(idx):
    return np.tile(idx.reshape(-1, 16).T, (8, 1)).astype(np.uint16)


def unstriped(offs):
    return offs[:16].T.reshape(-1).astype(np.int64)


def striped8(idx):
    return np.concatenate([x.reshape(-1, 16).T for x in idx]).astype(np.uint16)


def runs(offs, k):
    lists = np.stack([offs[16 * r : 16 * r + 16].T.reshape(-1) for r in range(8)]).astype(np.int64)
    return lists[np.arange(k) % 512 // 64]


def pack_weight(w):
    k, n = w.shape
    w = f64(np.asarray(w, np.float32).astype(ml_dtypes.bfloat16)).reshape(k // 32, 32, n)
    amax = np.abs(w).max(1)
    byte = np.clip(np.where(amax > 0, np.frexp(amax)[1] - 1 + 127 - 7, 1), 1, 254)
    scaled = (w * np.exp2(127.0 - byte)[:, None, :]).reshape(k, n).astype(np.float32)
    words = np.ascontiguousarray(scaled.reshape(k // 512, 128, 4, n).transpose(0, 1, 3, 2)).astype(ml_dtypes.float8_e4m3fn).view(np.uint8)
    return words, np.ascontiguousarray(byte.astype(np.uint8).reshape(k // 512, 16, n))


def unpack_weight(words, scales):
    g, p, n, _ = words.shape
    vals = np.ascontiguousarray(words).view(ml_dtypes.float8_e4m3fn).astype(np.float64) * np.repeat(np.exp2(scales.astype(np.float64) - 127.0), 8, axis=1)[..., None]
    return vals.transpose(0, 1, 3, 2).reshape(g * 512, n)


def sigmoid(v):
    return 1.0 / (1.0 + np.exp(-np.maximum(v, -700.0)))


K, T, S, H, G = 512, 1024, 256, 512, 2048


def setup_inputs():
    n = np.random.standard_normal
    s = mx_kscale(K)[:, None]
    packed_xT = pack_weight(n((K, T)) * s)
    packed_dT = pack_weight(n((K, G)) / s)
    return {
        "x_words": packed_xT[0],
        "x_scales": packed_xT[1],
        "w1": (n((K, H)) / np.sqrt(2 * K) / s).astype(np.float32),
        "w2": (n((K, H)) / np.sqrt(2 * K) / s).astype(np.float32),
        "gs": (np.random.uniform(0.5, 1.5, (K, 1)) * s).astype(np.float32),
        "d_words": packed_dT[0],
        "d_scales": packed_dT[1],
        "sl": np.random.uniform(1.0, 2.0, (H, 1)).astype(np.float32),
        "th": (0.5 * n((H, 1))).astype(np.float32),
        "offs": striped8(np.random.randint(0, T, (8, S))),
        "hz": striped8(np.random.randint(0, T, (8, S))),
        "k1": striped8(np.random.randint(0, G, (8, H))),
        "n1": striped(np.random.permutation(S)),
        "n2": striped(np.random.permutation(S)),
    }


def reference(x_words, x_scales, w1, w2, gs, d_words, d_scales, sl, th, offs, hz, k1, n1, n2):
    d_k1 = unpack_weight(d_words, d_scales)[np.arange(K)[:, None], runs(k1, K)]
    xq = unpack_weight(x_words, x_scales)[np.arange(K)[:, None], runs(offs, K)]
    x_hz = unpack_weight(x_words, x_scales)[np.arange(K)[:, None], runs(hz, K)]
    y = mxq(f64(w1), 0, "e4m3").T @ xq + mxq(f64(w2), 0, "e4m3").T @ x_hz
    z = f64(gs) * y
    h = 0.0625 * ((d_k1.T @ mxq(z, 0, "e4m3")))
    ds = np.zeros((H, S))
    ds[:, unstriped(n1)] = h
    sg = sigmoid(f64(sl) * (ds[:, unstriped(n2)] - f64(th)))
    return h * sg

@@ -1,0 +1,232 @@
+from contextlib import ExitStack
+
+import concourse.mybir as mybir
+from concourse.masks import make_identity
+
+K, T, S, H, G = 512, 1024, 256, 512, 2048
+FLOPS = 2 * (2 * K * H * S) + 2 * K * H * S
+
+F32 = mybir.dt.float32
+BF16 = mybir.dt.bfloat16
+I32 = mybir.dt.int32
+U32 = mybir.dt.uint32
+U16 = mybir.dt.uint16
+U8 = mybir.dt.uint8
+FP8X4 = mybir.dt.float8_e4m3fn_x4
+ALU = mybir.AluOpType
+ACT = mybir.ActivationFunctionType
+
+P = 128
+PACK = 4
+LIST_ROWS = 16
+HALF = S // 2
+WINDOW = 2 * S
+W1_SCALAR_M = 64
+W2_SCALAR_M = 40
+
+
+def tile_picked_dhqierl_none_p_kernel(
+    tc, x_words, x_scales, w1, w2, gs, d_words, d_scales, sl, th, offs, hz, k1, n1, n2, out
+):
+    nc = tc.nc
+    with ExitStack() as ctx:
+        lists = ctx.enter_context(tc.tile_pool(name="lists", bufs=1))
+        keep = ctx.enter_context(tc.tile_pool(name="keep", bufs=1))
+        y_psum = ctx.enter_context(tc.psum_pool(name="y_psum", bufs=1))
+        h_psum = ctx.enter_context(tc.psum_pool(name="h_psum", bufs=6))
+
+        def load_list(name, source):
+            tile = lists.tile(list(source.shape), U16, name=name)
+            nc.sync.dma_start(tile[:], source)
+            return tile
+
+        def entries(tile, first, count):
+            return tile[:, first // LIST_ROWS : (first + count) // LIST_ROWS]
+
+        def load_scale_rows(name, source, clearing_engine):
+            columns = source.shape[2]
+            tile = keep.tile([P, columns], U8, name=name, align_bytes=64)
+            clearing_engine.memset(tile[:].bitcast(I32), 0)
+            nc.scalar.dma_start(tile[0:P:8, :].bitcast(I32), source[0].bitcast(I32))
+            return tile
+
+        def load_words(name, source):
+            columns = source.shape[2]
+            tile = keep.tile([P, columns], I32, name=name, align_bytes=64)
+            nc.sync.dma_start(tile[:], source[0].rearrange("p c r -> p (c r)").bitcast(I32))
+            return tile
+
+        def load_weight(name, source):
+            tile = keep.tile([P, PACK, H], F32, name=name, align_bytes=64)
+            nc.sync.dma_start(tile[:], source.rearrange("(p j) c -> p j c", j=PACK))
+            return tile
+
+        x_scale_rows = load_scale_rows("x_scale_rows", x_scales, nc.vector)
+        d_scale_rows = load_scale_rows("d_scale_rows", d_scales, nc.gpsimd)
+        offs_list = load_list("offs_list", offs)
+        hz_list = load_list("hz_list", hz)
+        k1_list = load_list("k1_list", k1)
+        n1_list = load_list("n1_list", n1)
+        n2_list = load_list("n2_list", n2)
+        w1_raw = load_weight("w1_raw", w1)
+        w2_raw = load_weight("w2_raw", w2)
+        x_table = load_words("x_table", x_words)
+        d_table = load_words("d_table", d_words)
+
+        blocks = H // P
+        row_values = keep.tile([P, P], F32)
+        nc.gpsimd.memset(row_values[:], 0.0)
+        nc.gpsimd.dma_start(row_values[0:blocks, :], sl.rearrange("(u p) o -> u (p o)", p=P))
+        nc.gpsimd.dma_start(row_values[32 : 32 + blocks, :], th.rearrange("(u p) o -> u (p o)", p=P))
+        gain = keep.tile([P, PACK], F32)
+        nc.gpsimd.dma_start(gain[:], gs.rearrange("(p t) o -> p (t o)", t=PACK))
+        identity = keep.tile([P, P], F32)
+        make_identity(nc, identity[:])
+        turned = h_psum.tile([P, P], F32, name="turned", tag="h_bank")
+        nc.tensor.transpose(turned[:], row_values[:], identity[:])
+        slope = keep.tile([P, blocks], F32)
+        nc.vector.tensor_copy(slope[:], turned[:, 0:blocks])
+        bias = keep.tile([P, blocks], F32)
+        nc.vector.scalar_tensor_tensor(bias[:], turned[:, 32 : 32 + blocks], -1.0, slope[:], ALU.mult, ALU.mult)
+
+        def pick_scales(name, rows, place_lists, moving_engine):
+            count = sum(LIST_ROWS * place_list.shape[1] for place_list in place_lists)
+            picked = keep.tile([P, count], U8, name=name + "_picked", align_bytes=64)
+            first = 0
+            for place_list in place_lists:
+                length = LIST_ROWS * place_list.shape[1]
+                nc.vector.tensor_copy(picked[:, first : first + length], rows[:].indirect(place_list[:]))
+                first = first + length
+            plane = keep.tile([P, count], U8, name=name, align_bytes=64)
+            nc.vector.tensor_copy(plane[:].bitcast(I32), picked[:].bitcast(I32))
+            for j in range(1, 4):
+                moving_engine.dma_start(plane[j:P:32, :].bitcast(I32), picked[8 * j : P : 32, :].bitcast(I32))
+            return plane
+
+        x_plane = pick_scales("x_plane", x_scale_rows, (offs_list, hz_list), nc.scalar)
+        d_plane = pick_scales("d_plane", d_scale_rows, (k1_list,), nc.gpsimd)
+
+        def round_weight(name, raw, scalar_m):
+            grouped = keep.tile([P, PACK * H], BF16, name=name, align_bytes=64)
+            source = raw[:].rearrange("p j (m t) -> p m j t", t=PACK)
+            target = grouped[:].rearrange("p (t m j) -> p m j t", t=PACK, j=PACK)
+            nc.scalar.copy(target[:, :scalar_m], source[:, :scalar_m])
+            nc.vector.tensor_copy(target[:, scalar_m:], source[:, scalar_m:])
+            return grouped
+
+        def quantize(name, grouped):
+            columns = grouped.shape[1] // PACK
+            codes = keep.tile([P, columns], U32, name=name + "_codes", align_bytes=64)
+            scales = keep.tile([P, columns], U8, name=name + "_scales", align_bytes=64)
+            nc.vector.quantize_mx(out=codes[:].bitcast(FP8X4), scales=scales[:], in_=grouped[:])
+            return codes, scales
+
+        w1_grouped = round_weight("w1_grouped", w1_raw, W1_SCALAR_M)
+        w1_mx = quantize("w1", w1_grouped)
+        w2_grouped = round_weight("w2_grouped", w2_raw, W2_SCALAR_M)
+        w2_mx = quantize("w2", w2_grouped)
+
+        def pick_words(name, table, offsets, count):
+            tile = keep.tile([P, count], U32, name=name, align_bytes=64)
+            nc.vector.tensor_copy(tile[:], table[:].bitcast(U32).indirect(offsets))
+            return tile
+
+        y_banks = []
+        for half in range(2):
+            bank = y_psum.tile([P, PACK, HALF], F32, name="y%d" % half)
+            y_banks.append(bank)
+            for which, (place_list, (codes, scales)) in enumerate(((offs_list, w1_mx), (hz_list, w2_mx))):
+                first = half * HALF
+                picked = pick_words("x%d_%d" % (which, half), x_table, entries(place_list, first, HALF), HALF)
+                plane = x_plane[:, which * S + first : which * S + first + HALF]
+                for t in range(PACK):
+                    columns = slice(t * P, (t + 1) * P)
+                    nc.tensor.matmul_mx(
+                        out=bank[:, t, :],
+                        lhsT=codes[:, columns].bitcast(FP8X4),
+                        lhsT_scale=scales[:, columns],
+                        rhs=picked[:].bitcast(FP8X4),
+                        rhs_scale=plane,
+                        start=(which == 0 and t == 0),
+                        stop=(which == 1 and t == PACK - 1),
+                    )
+
+        def weigh(half):
+            z = keep.tile([P, HALF * PACK], BF16, name="z%d" % half, align_bytes=64)
+            nc.vector.tensor_tensor(
+                z[:].rearrange("p (j t) -> p j t", t=PACK),
+                y_banks[half][:].rearrange("p t j -> p j t"),
+                gain[:].unsqueeze(1).to_broadcast([P, HALF, PACK]),
+                ALU.mult,
+            )
+            return z
+
+        def pick_codewords(pair):
+            return pick_words("d%d" % pair, d_table, entries(k1_list, pair * 2 * P, 2 * P), 2 * P)
+
+        h = [keep.tile([P, S], F32, name="h%d" % u) for u in range(H // P)]
+        ds = [keep.tile([P, WINDOW], F32, name="ds%d" % u) for u in range(H // P)]
+        codewords = []
+        z_mx = []
+
+        def product(u, half):
+            bank = h_psum.tile([P, HALF], F32, name="h_bank", tag="h_bank")
+            columns = slice((u % 2) * P, (u % 2 + 1) * P)
+            codes, scales = z_mx[half]
+            nc.tensor.matmul_mx(
+                out=bank[:],
+                lhsT=codewords[u // 2][:, columns].bitcast(FP8X4),
+                lhsT_scale=d_plane[:, u * P : (u + 1) * P],
+                rhs=codes[:].bitcast(FP8X4),
+                rhs_scale=scales[:],
+                start=True,
+                stop=True,
+            )
+            places = slice(half * HALF, (half + 1) * HALF)
+            nc.vector.tensor_scalar(h[u][:, places], bank[:], 0.0625, None, ALU.mult)
+
+        def send(u, half):
+            places = slice(half * HALF, (half + 1) * HALF)
+            nc.scalar.activation(
+                out=ds[u][:].indirect(entries(n1_list, half * HALF, HALF)), in_=h[u][:, places], func=ACT.Copy
+            )
+
+        def fetch(u):
+            sg = keep.tile([P, S], F32, name="sg%d" % u)
+            nc.scalar.activation(
+                out=sg[:],
+                in_=ds[u][:].indirect(n2_list[:]),
+                func=ACT.Sigmoid,
+                scale=slope[:, u : u + 1],
+                bias=bias[:, u : u + 1],
+            )
+            result = keep.tile([P, S], F32, name="result%d" % u)
+            nc.vector.tensor_tensor(result[:], h[u][:], sg[:], ALU.mult)
+            nc.sync.dma_start(out[u * P : (u + 1) * P, :], result[:])
+
+        z_first = weigh(0)
+        codewords.append(pick_codewords(0))
+        z_mx.append(quantize("z0", z_first))
+        z_second = weigh(1)
+        product(0, 0)
+        z_mx.append(quantize("z1", z_second))
+        product(1, 0)
+        product(0, 1)
+        product(1, 1)
+        codewords.append(pick_codewords(1))
+        for u in (2, 3):
+            for half in range(2):
+                product(u, half)
+
+        send(0, 0)
+        send(1, 0)
+        send(0, 1)
+        send(1, 1)
+        fetch(0)
+        send(2, 0)
+        send(2, 1)
+        fetch(1)
+        send(3, 0)
+        send(3, 1)
+        fetch(2)
+        fetch(3)

@@ -63,6 +63,11 @@ def tile_picked_dhqierl_none_p_kernel(
 
         x_scale_rows = load_scale_rows("x_scale_rows", x_scales, nc.vector)
         d_scale_rows = load_scale_rows("d_scale_rows", d_scales, nc.gpsimd)
+        warm_in = keep.tile([P, 1], F32)
+        nc.vector.memset(warm_in[:], 0.0)
+        warm_out = keep.tile([P, 1], F32)
+        nc.scalar.activation(out=warm_out[:], in_=warm_in[:], func=ACT.Sigmoid)
+
         offs_list = load_list("offs_list", offs)
         hz_list = load_list("hz_list", hz)
         k1_list = load_list("k1_list", k1)

@@ -1,10 +1,9 @@
 from contextlib import ExitStack
 
 import concourse.mybir as mybir
-from concourse.masks import make_identity
 
-K, T, S, H, G = 512, 1024, 256, 512, 2048
-FLOPS = 2 * (2 * K * H * S) + 2 * K * H * S
+K, S, H = 512, 256, 512
+FLOPS = 3 * 2 * K * H * S
 
 F32 = mybir.dt.float32
 BF16 = mybir.dt.bfloat16
@@ -18,11 +17,17 @@ ACT = mybir.ActivationFunctionType
 
 P = 128
 PACK = 4
+QUADRANT = 32
+BLOCK_PARTITIONS = 8
 LIST_ROWS = 16
+BLOCKS = H // P
 HALF = S // 2
 WINDOW = 2 * S
-W1_SCALAR_M = 64
-W2_SCALAR_M = 40
+H_SCALE = 0.0625
+W1_SCALAR_GROUPS = 92
+W2_SCALAR_GROUPS = 40
+H_BANKS = 5
+THRESHOLD_COLUMN = 8
 
 
 def tile_picked_dhqierl_none_p_kernel(
@@ -33,205 +38,221 @@ def tile_picked_dhqierl_none_p_kernel(
         lists = ctx.enter_context(tc.tile_pool(name="lists", bufs=1))
         keep = ctx.enter_context(tc.tile_pool(name="keep", bufs=1))
         y_psum = ctx.enter_context(tc.psum_pool(name="y_psum", bufs=1))
-        h_psum = ctx.enter_context(tc.psum_pool(name="h_psum", bufs=6))
+        h_psum = ctx.enter_context(tc.psum_pool(name="h_psum", bufs=H_BANKS))
 
         def load_list(name, source):
             tile = lists.tile(list(source.shape), U16, name=name)
             nc.sync.dma_start(tile[:], source)
             return tile
 
-        def entries(tile, first, count):
-            return tile[:, first // LIST_ROWS : (first + count) // LIST_ROWS]
+        def entries(list_tile, first, count):
+            return list_tile[:, first // LIST_ROWS : (first + count) // LIST_ROWS]
 
-        def load_scale_rows(name, source, clearing_engine):
-            columns = source.shape[2]
-            tile = keep.tile([P, columns], U8, name=name, align_bytes=64)
-            clearing_engine.memset(tile[:].bitcast(I32), 0)
-            nc.scalar.dma_start(tile[0:P:8, :].bitcast(I32), source[0].bitcast(I32))
+        def load_scale_rows(name, tag, source, queue):
+            tile = keep.tile([P, source.shape[2]], U8, name=name, tag=tag, align_bytes=64)
+            nc.vector.memset(tile[:].bitcast(I32), 0)
+            queue.dma_start(tile[0:P:BLOCK_PARTITIONS, :].bitcast(I32), source[0].bitcast(I32))
             return tile
 
-        def load_words(name, source):
-            columns = source.shape[2]
-            tile = keep.tile([P, columns], I32, name=name, align_bytes=64)
+        def load_words(name, tag, source):
+            tile = keep.tile([P, source.shape[2]], I32, name=name, tag=tag, align_bytes=64)
             nc.sync.dma_start(tile[:], source[0].rearrange("p c r -> p (c r)").bitcast(I32))
             return tile
 
         def load_weight(name, source):
-            tile = keep.tile([P, PACK, H], F32, name=name, align_bytes=64)
+            tile = keep.tile([P, PACK, H], F32, name=name, tag=name, align_bytes=64)
             nc.sync.dma_start(tile[:], source.rearrange("(p j) c -> p j c", j=PACK))
             return tile
 
-        x_scale_rows = load_scale_rows("x_scale_rows", x_scales, nc.vector)
-        d_scale_rows = load_scale_rows("d_scale_rows", d_scales, nc.gpsimd)
+        x_scale_rows = load_scale_rows("x_scale_rows", "x_rows_then_d_table", x_scales, nc.scalar)
+        d_scale_rows = load_scale_rows("d_scale_rows", "d_scale_rows", d_scales, nc.sync)
+        x_table = load_words("x_table", "x_table", x_words)
+        offs_list = load_list("offs_list", offs)
+        hz_list = load_list("hz_list", hz)
+        k1_list = load_list("k1_list", k1)
+        n1_list = load_list("n1_list", n1)
+        w1_raw = load_weight("w1_raw", w1)
+        n2_list = load_list("n2_list", n2)
+        gain = keep.tile([P, PACK], F32)
+        nc.sync.dma_start(gain[:], gs.rearrange("(p t) o -> p (t o)", t=PACK))
+        w2_raw = load_weight("w2_raw", w2)
+
         warm_in = keep.tile([P, 1], F32)
         nc.vector.memset(warm_in[:], 0.0)
         warm_out = keep.tile([P, 1], F32)
         nc.scalar.activation(out=warm_out[:], in_=warm_in[:], func=ACT.Sigmoid)
 
-        offs_list = load_list("offs_list", offs)
-        hz_list = load_list("hz_list", hz)
-        k1_list = load_list("k1_list", k1)
-        n1_list = load_list("n1_list", n1)
-        n2_list = load_list("n2_list", n2)
-        w1_raw = load_weight("w1_raw", w1)
-        w2_raw = load_weight("w2_raw", w2)
-        x_table = load_words("x_table", x_words)
-        d_table = load_words("d_table", d_words)
-
-        blocks = H // P
-        row_values = keep.tile([P, P], F32)
-        nc.gpsimd.memset(row_values[:], 0.0)
-        nc.gpsimd.dma_start(row_values[0:blocks, :], sl.rearrange("(u p) o -> u (p o)", p=P))
-        nc.gpsimd.dma_start(row_values[32 : 32 + blocks, :], th.rearrange("(u p) o -> u (p o)", p=P))
-        gain = keep.tile([P, PACK], F32)
-        nc.gpsimd.dma_start(gain[:], gs.rearrange("(p t) o -> p (t o)", t=PACK))
-        identity = keep.tile([P, P], F32)
-        make_identity(nc, identity[:])
-        turned = h_psum.tile([P, P], F32, name="turned", tag="h_bank")
-        nc.tensor.transpose(turned[:], row_values[:], identity[:])
-        slope = keep.tile([P, blocks], F32)
-        nc.vector.tensor_copy(slope[:], turned[:, 0:blocks])
-        bias = keep.tile([P, blocks], F32)
-        nc.vector.scalar_tensor_tensor(bias[:], turned[:, 32 : 32 + blocks], -1.0, slope[:], ALU.mult, ALU.mult)
-
-        def pick_scales(name, rows, place_lists, moving_engine):
-            count = sum(LIST_ROWS * place_list.shape[1] for place_list in place_lists)
-            picked = keep.tile([P, count], U8, name=name + "_picked", align_bytes=64)
+        def pick_bytes(name, scale_rows, list_tiles):
+            lengths = [LIST_ROWS * list_tile.shape[1] for list_tile in list_tiles]
+            picked = keep.tile([P, sum(lengths)], U8, name=name, tag=name, align_bytes=64)
             first = 0
-            for place_list in place_lists:
-                length = LIST_ROWS * place_list.shape[1]
-                nc.vector.tensor_copy(picked[:, first : first + length], rows[:].indirect(place_list[:]))
+            for list_tile, length in zip(list_tiles, lengths):
+                nc.vector.tensor_copy(picked[:, first : first + length], scale_rows[:].indirect(list_tile[:]))
                 first = first + length
-            plane = keep.tile([P, count], U8, name=name, align_bytes=64)
-            nc.vector.tensor_copy(plane[:].bitcast(I32), picked[:].bitcast(I32))
-            for j in range(1, 4):
-                moving_engine.dma_start(plane[j:P:32, :].bitcast(I32), picked[8 * j : P : 32, :].bitcast(I32))
-            return plane
+            return picked
 
-        x_plane = pick_scales("x_plane", x_scale_rows, (offs_list, hz_list), nc.scalar)
-        d_plane = pick_scales("d_plane", d_scale_rows, (k1_list,), nc.gpsimd)
+        def pick_columns(half, tag):
+            picked = keep.tile([P, 2 * HALF], U32, name="x_picked%d" % half, tag=tag, align_bytes=64)
+            for which, list_tile in enumerate((offs_list, hz_list)):
+                nc.vector.tensor_copy(
+                    picked[:, which * HALF : (which + 1) * HALF],
+                    x_table[:].bitcast(U32).indirect(entries(list_tile, half * HALF, HALF)),
+                )
+            return picked
 
-        def round_weight(name, raw, scalar_m):
+        def move_rows(plane, picked, rows):
+            for j in rows:
+                nc.sync.dma_start(
+                    plane[j:P:QUADRANT, :].bitcast(I32), picked[BLOCK_PARTITIONS * j : P : QUADRANT, :].bitcast(I32)
+                )
+
+        x_plane = keep.tile([P, 2 * S], U8, align_bytes=64)
+        nc.gpsimd.memset(x_plane[:].bitcast(I32), 0)
+        x_bytes = pick_bytes("x_bytes", x_scale_rows, (offs_list, hz_list))
+        move_rows(x_plane, x_bytes, range(PACK))
+        d_table = load_words("d_table", "x_rows_then_d_table", d_words)
+        x_first = pick_columns(0, "x_first")
+        d_bytes = pick_bytes("d_bytes", d_scale_rows, (k1_list,))
+        d_plane = keep.tile([P, H], U8, align_bytes=64)
+        nc.vector.tensor_copy(d_plane[:].bitcast(I32), d_bytes[:].bitcast(I32))
+        move_rows(d_plane, d_bytes, range(1, PACK))
+
+        def round_weight(name, raw, scalar_groups):
             grouped = keep.tile([P, PACK * H], BF16, name=name, align_bytes=64)
             source = raw[:].rearrange("p j (m t) -> p m j t", t=PACK)
             target = grouped[:].rearrange("p (t m j) -> p m j t", t=PACK, j=PACK)
-            nc.scalar.copy(target[:, :scalar_m], source[:, :scalar_m])
-            nc.vector.tensor_copy(target[:, scalar_m:], source[:, scalar_m:])
+            nc.scalar.copy(target[:, :scalar_groups], source[:, :scalar_groups])
+            nc.vector.tensor_copy(target[:, scalar_groups:], source[:, scalar_groups:])
             return grouped
 
-        def quantize(name, grouped):
+        def quantize(name, codes_tag, grouped, pieces):
             columns = grouped.shape[1] // PACK
-            codes = keep.tile([P, columns], U32, name=name + "_codes", align_bytes=64)
+            codes = keep.tile([P, columns], U32, name=name + "_codes", tag=codes_tag, align_bytes=64)
             scales = keep.tile([P, columns], U8, name=name + "_scales", align_bytes=64)
-            nc.vector.quantize_mx(out=codes[:].bitcast(FP8X4), scales=scales[:], in_=grouped[:])
+            width = columns // pieces
+            for first in range(0, columns, width):
+                nc.vector.quantize_mx(
+                    out=codes[:, first : first + width].bitcast(FP8X4),
+                    scales=scales[:, first : first + width],
+                    in_=grouped[:, PACK * first : PACK * (first + width)],
+                )
             return codes, scales
 
-        w1_grouped = round_weight("w1_grouped", w1_raw, W1_SCALAR_M)
-        w1_mx = quantize("w1", w1_grouped)
-        w2_grouped = round_weight("w2_grouped", w2_raw, W2_SCALAR_M)
-        w2_mx = quantize("w2", w2_grouped)
+        y_banks = [y_psum.tile([P, PACK, HALF], F32, name="y%d" % half) for half in range(2)]
 
-        def pick_words(name, table, offsets, count):
-            tile = keep.tile([P, count], U32, name=name, align_bytes=64)
-            nc.vector.tensor_copy(tile[:], table[:].bitcast(U32).indirect(offsets))
-            return tile
-
-        y_banks = []
-        for half in range(2):
-            bank = y_psum.tile([P, PACK, HALF], F32, name="y%d" % half)
-            y_banks.append(bank)
-            for which, (place_list, (codes, scales)) in enumerate(((offs_list, w1_mx), (hz_list, w2_mx))):
-                first = half * HALF
-                picked = pick_words("x%d_%d" % (which, half), x_table, entries(place_list, first, HALF), HALF)
-                plane = x_plane[:, which * S + first : which * S + first + HALF]
+        def project(half, picked):
+            for which, (codes, scales) in enumerate((w1_mx, w2_mx)):
+                first = which * S + half * HALF
                 for t in range(PACK):
                     columns = slice(t * P, (t + 1) * P)
                     nc.tensor.matmul_mx(
-                        out=bank[:, t, :],
+                        out=y_banks[half][:, t, :],
                         lhsT=codes[:, columns].bitcast(FP8X4),
                         lhsT_scale=scales[:, columns],
-                        rhs=picked[:].bitcast(FP8X4),
-                        rhs_scale=plane,
+                        rhs=picked[:, which * HALF : (which + 1) * HALF].bitcast(FP8X4),
+                        rhs_scale=x_plane[:, first : first + HALF],
                         start=(which == 0 and t == 0),
                         stop=(which == 1 and t == PACK - 1),
                     )
 
+        w1_mx = quantize("w1", "w1_codes", round_weight("w1_grouped", w1_raw, W1_SCALAR_GROUPS), 1)
+        w2_mx = quantize("w2", "w2_codes", round_weight("w2_grouped", w2_raw, W2_SCALAR_GROUPS), PACK)
+        project(0, x_first)
+        project(1, pick_columns(1, "w2_raw"))
+
+        row_values = keep.tile([P, 2 * THRESHOLD_COLUMN], F32, tag="w1_raw", align_bytes=64)
+        slope = row_values[:, 0:BLOCKS]
+        threshold = row_values[:, THRESHOLD_COLUMN : THRESHOLD_COLUMN + BLOCKS]
+        with nc.allow_non_contiguous_dma(reason="one value a partition and row block"):
+            nc.sync.dma_start(slope, sl.rearrange("(u p) o -> p (u o)", p=P))
+            nc.sync.dma_start(threshold, th.rearrange("(u p) o -> p (u o)", p=P))
+        slope_times_threshold = keep.tile([P, BLOCKS], F32)
+        nc.gpsimd.tensor_tensor(slope_times_threshold[:], slope, threshold, ALU.mult)
+        bias = keep.tile([P, BLOCKS], F32)
+        nc.gpsimd.tensor_scalar(bias[:], slope_times_threshold[:], -1.0, 0.0, ALU.mult, ALU.add)
+
         def weigh(half):
-            z = keep.tile([P, HALF * PACK], BF16, name="z%d" % half, align_bytes=64)
+            z = keep.tile([P, HALF * PACK], BF16, name="z%d" % half, tag="z", align_bytes=64)
             nc.vector.tensor_tensor(
-                z[:].rearrange("p (j t) -> p j t", t=PACK),
-                y_banks[half][:].rearrange("p t j -> p j t"),
-                gain[:].unsqueeze(1).to_broadcast([P, HALF, PACK]),
+                z[:].rearrange("p (c i t) -> p c t i", i=PACK, t=PACK),
+                y_banks[half][:].rearrange("p t (c i) -> p c t i", i=PACK),
+                gain[:].unsqueeze(1).unsqueeze(3).to_broadcast([P, HALF // PACK, PACK, PACK]),
                 ALU.mult,
             )
             return z
 
-        def pick_codewords(pair):
-            return pick_words("d%d" % pair, d_table, entries(k1_list, pair * 2 * P, 2 * P), 2 * P)
+        def pick_codewords(pair, tag):
+            picked = keep.tile([P, 2 * P], U32, name="d%d" % pair, tag=tag, align_bytes=64)
+            nc.vector.tensor_copy(picked[:], d_table[:].bitcast(U32).indirect(entries(k1_list, pair * 2 * P, 2 * P)))
+            return picked
 
-        h = [keep.tile([P, S], F32, name="h%d" % u) for u in range(H // P)]
-        ds = [keep.tile([P, WINDOW], F32, name="ds%d" % u) for u in range(H // P)]
+        h = [keep.tile([P, 2, S], F32, name="h%d" % pair) for pair in range(2)]
+        ds = [keep.tile([P, WINDOW], F32, name="ds%d" % u) for u in range(BLOCKS)]
         codewords = []
         z_mx = []
 
-        def product(u, half):
-            bank = h_psum.tile([P, HALF], F32, name="h_bank", tag="h_bank")
-            columns = slice((u % 2) * P, (u % 2 + 1) * P)
+        def multiply(target, u, half):
             codes, scales = z_mx[half]
             nc.tensor.matmul_mx(
-                out=bank[:],
-                lhsT=codewords[u // 2][:, columns].bitcast(FP8X4),
+                out=target,
+                lhsT=codewords[u // 2][:, (u % 2) * P : (u % 2 + 1) * P].bitcast(FP8X4),
                 lhsT_scale=d_plane[:, u * P : (u + 1) * P],
                 rhs=codes[:].bitcast(FP8X4),
                 rhs_scale=scales[:],
                 start=True,
                 stop=True,
             )
-            places = slice(half * HALF, (half + 1) * HALF)
-            nc.vector.tensor_scalar(h[u][:, places], bank[:], 0.0625, None, ALU.mult)
+
+        def first_products():
+            for u in range(2):
+                bank = h_psum.tile([P, HALF], F32, name="h_first", tag="h_bank")
+                multiply(bank[:], u, 0)
+                nc.scalar.activation(out=h[0][:, u, 0:HALF], in_=bank[:], func=ACT.Copy, scale=H_SCALE)
+
+        def pair_products(pair, half):
+            bank = h_psum.tile([P, 2, HALF], F32, name="h_pair", tag="h_bank")
+            for member in range(2):
+                multiply(bank[:, member, :], 2 * pair + member, half)
+            nc.vector.tensor_scalar(h[pair][:, :, half * HALF : (half + 1) * HALF], bank[:], H_SCALE, None, ALU.mult)
 
         def send(u, half):
-            places = slice(half * HALF, (half + 1) * HALF)
             nc.scalar.activation(
-                out=ds[u][:].indirect(entries(n1_list, half * HALF, HALF)), in_=h[u][:, places], func=ACT.Copy
+                out=ds[u][:].indirect(entries(n1_list, half * HALF, HALF)),
+                in_=h[u // 2][:, u % 2, half * HALF : (half + 1) * HALF],
+                func=ACT.Copy,
             )
 
-        def fetch(u):
-            sg = keep.tile([P, S], F32, name="sg%d" % u)
+        def fetch(u, first, count):
+            places = slice(first, first + count)
+            sg = keep.tile([P, count], F32, name="sg%d_%d" % (u, first))
             nc.scalar.activation(
                 out=sg[:],
-                in_=ds[u][:].indirect(n2_list[:]),
+                in_=ds[u][:].indirect(entries(n2_list, first, count)),
                 func=ACT.Sigmoid,
                 scale=slope[:, u : u + 1],
                 bias=bias[:, u : u + 1],
             )
-            result = keep.tile([P, S], F32, name="result%d" % u)
-            nc.vector.tensor_tensor(result[:], h[u][:], sg[:], ALU.mult)
-            nc.sync.dma_start(out[u * P : (u + 1) * P, :], result[:])
+            result = keep.tile([P, count], F32, name="result%d_%d" % (u, first))
+            nc.vector.tensor_tensor(result[:], h[u // 2][:, u % 2, places], sg[:], ALU.mult)
+            nc.sync.dma_start(out[u * P : (u + 1) * P, places], result[:])
 
         z_first = weigh(0)
-        codewords.append(pick_codewords(0))
-        z_mx.append(quantize("z0", z_first))
+        codewords.append(pick_codewords(0, "d0"))
+        z_mx.append(quantize("z0", "d_bytes", z_first, 1))
         z_second = weigh(1)
-        product(0, 0)
-        z_mx.append(quantize("z1", z_second))
-        product(1, 0)
-        product(0, 1)
-        product(1, 1)
-        codewords.append(pick_codewords(1))
-        for u in (2, 3):
-            for half in range(2):
-                product(u, half)
+        first_products()
+        z_mx.append(quantize("z1", "z1_codes", z_second, 1))
+        pair_products(0, 1)
+        codewords.append(pick_codewords(1, "z"))
+        pair_products(1, 0)
+        pair_products(1, 1)
 
-        send(0, 0)
-        send(1, 0)
-        send(0, 1)
-        send(1, 1)
-        fetch(0)
-        send(2, 0)
-        send(2, 1)
-        fetch(1)
-        send(3, 0)
-        send(3, 1)
-        fetch(2)
-        fetch(3)
+        for pair in range(2):
+            members = (2 * pair, 2 * pair + 1)
+            for half in range(2):
+                for u in members:
+                    send(u, half)
+            for u in members:
+                width = HALF if u == BLOCKS - 1 else S
+                for first in range(0, S, width):
+                    fetch(u, first, width)

from contextlib import ExitStack

import concourse.mybir as mybir

K, S, H = 512, 256, 512
FLOPS = 3 * 2 * K * H * S

F32 = mybir.dt.float32
BF16 = mybir.dt.bfloat16
I32 = mybir.dt.int32
U32 = mybir.dt.uint32
U16 = mybir.dt.uint16
U8 = mybir.dt.uint8
FP8X4 = mybir.dt.float8_e4m3fn_x4
ALU = mybir.AluOpType
ACT = mybir.ActivationFunctionType

P = 128
PACK = 4
QUADRANT = 32
BLOCK_PARTITIONS = 8
LIST_ROWS = 16
BLOCKS = H // P
HALF = S // 2
WINDOW = 2 * S
H_SCALE = 0.0625
W1_SCALAR_GROUPS = 92
W2_SCALAR_GROUPS = 40
H_BANKS = 5
THRESHOLD_COLUMN = 8


def tile_picked_dhqierl_none_p_kernel(
    tc, x_words, x_scales, w1, w2, gs, d_words, d_scales, sl, th, offs, hz, k1, n1, n2, out
):
    nc = tc.nc
    with ExitStack() as ctx:
        lists = ctx.enter_context(tc.tile_pool(name="lists", bufs=1))
        keep = ctx.enter_context(tc.tile_pool(name="keep", bufs=1))
        y_psum = ctx.enter_context(tc.psum_pool(name="y_psum", bufs=1))
        h_psum = ctx.enter_context(tc.psum_pool(name="h_psum", bufs=H_BANKS))

        def load_list(name, source):
            tile = lists.tile(list(source.shape), U16, name=name)
            nc.sync.dma_start(tile[:], source)
            return tile

        def entries(list_tile, first, count):
            return list_tile[:, first // LIST_ROWS : (first + count) // LIST_ROWS]

        def load_scale_rows(name, tag, source, queue):
            tile = keep.tile([P, source.shape[2]], U8, name=name, tag=tag, align_bytes=64)
            nc.vector.memset(tile[:].bitcast(I32), 0)
            queue.dma_start(tile[0:P:BLOCK_PARTITIONS, :].bitcast(I32), source[0].bitcast(I32))
            return tile

        def load_words(name, tag, source):
            tile = keep.tile([P, source.shape[2]], I32, name=name, tag=tag, align_bytes=64)
            nc.sync.dma_start(tile[:], source[0].rearrange("p c r -> p (c r)").bitcast(I32))
            return tile

        def load_weight(name, source):
            tile = keep.tile([P, PACK, H], F32, name=name, tag=name, align_bytes=64)
            nc.sync.dma_start(tile[:], source.rearrange("(p j) c -> p j c", j=PACK))
            return tile

        x_scale_rows = load_scale_rows("x_scale_rows", "x_rows_then_d_table", x_scales, nc.scalar)
        d_scale_rows = load_scale_rows("d_scale_rows", "d_scale_rows", d_scales, nc.sync)
        x_table = load_words("x_table", "x_table", x_words)
        offs_list = load_list("offs_list", offs)
        hz_list = load_list("hz_list", hz)
        k1_list = load_list("k1_list", k1)
        n1_list = load_list("n1_list", n1)
        w1_raw = load_weight("w1_raw", w1)
        n2_list = load_list("n2_list", n2)
        gain = keep.tile([P, PACK], F32)
        nc.sync.dma_start(gain[:], gs.rearrange("(p t) o -> p (t o)", t=PACK))
        w2_raw = load_weight("w2_raw", w2)

        warm_in = keep.tile([P, 1], F32)
        nc.vector.memset(warm_in[:], 0.0)
        warm_out = keep.tile([P, 1], F32)
        nc.scalar.activation(out=warm_out[:], in_=warm_in[:], func=ACT.Sigmoid)

        def pick_bytes(name, scale_rows, list_tiles):
            lengths = [LIST_ROWS * list_tile.shape[1] for list_tile in list_tiles]
            picked = keep.tile([P, sum(lengths)], U8, name=name, tag=name, align_bytes=64)
            first = 0
            for list_tile, length in zip(list_tiles, lengths):
                nc.vector.tensor_copy(picked[:, first : first + length], scale_rows[:].indirect(list_tile[:]))
                first = first + length
            return picked

        def pick_columns(half, tag):
            picked = keep.tile([P, 2 * HALF], U32, name="x_picked%d" % half, tag=tag, align_bytes=64)
            for which, list_tile in enumerate((offs_list, hz_list)):
                nc.vector.tensor_copy(
                    picked[:, which * HALF : (which + 1) * HALF],
                    x_table[:].bitcast(U32).indirect(entries(list_tile, half * HALF, HALF)),
                )
            return picked

        def move_rows(plane, picked, rows):
            for j in rows:
                nc.sync.dma_start(
                    plane[j:P:QUADRANT, :].bitcast(I32), picked[BLOCK_PARTITIONS * j : P : QUADRANT, :].bitcast(I32)
                )

        x_plane = keep.tile([P, 2 * S], U8, align_bytes=64)
        nc.gpsimd.memset(x_plane[:].bitcast(I32), 0)
        x_bytes = pick_bytes("x_bytes", x_scale_rows, (offs_list, hz_list))
        move_rows(x_plane, x_bytes, range(PACK))
        d_table = load_words("d_table", "x_rows_then_d_table", d_words)
        x_first = pick_columns(0, "x_first")
        d_bytes = pick_bytes("d_bytes", d_scale_rows, (k1_list,))
        d_plane = keep.tile([P, H], U8, align_bytes=64)
        nc.vector.tensor_copy(d_plane[:].bitcast(I32), d_bytes[:].bitcast(I32))
        move_rows(d_plane, d_bytes, range(1, PACK))

        def round_weight(name, raw, scalar_groups):
            grouped = keep.tile([P, PACK * H], BF16, name=name, align_bytes=64)
            source = raw[:].rearrange("p j (m t) -> p m j t", t=PACK)
            target = grouped[:].rearrange("p (t m j) -> p m j t", t=PACK, j=PACK)
            nc.scalar.copy(target[:, :scalar_groups], source[:, :scalar_groups])
            nc.vector.tensor_copy(target[:, scalar_groups:], source[:, scalar_groups:])
            return grouped

        def quantize(name, codes_tag, grouped, pieces):
            columns = grouped.shape[1] // PACK
            codes = keep.tile([P, columns], U32, name=name + "_codes", tag=codes_tag, align_bytes=64)
            scales = keep.tile([P, columns], U8, name=name + "_scales", align_bytes=64)
            width = columns // pieces
            for first in range(0, columns, width):
                nc.vector.quantize_mx(
                    out=codes[:, first : first + width].bitcast(FP8X4),
                    scales=scales[:, first : first + width],
                    in_=grouped[:, PACK * first : PACK * (first + width)],
                )
            return codes, scales

        y_banks = [y_psum.tile([P, PACK, HALF], F32, name="y%d" % half) for half in range(2)]

        def project(half, picked):
            for which, (codes, scales) in enumerate((w1_mx, w2_mx)):
                first = which * S + half * HALF
                for t in range(PACK):
                    columns = slice(t * P, (t + 1) * P)
                    nc.tensor.matmul_mx(
                        out=y_banks[half][:, t, :],
                        lhsT=codes[:, columns].bitcast(FP8X4),
                        lhsT_scale=scales[:, columns],
                        rhs=picked[:, which * HALF : (which + 1) * HALF].bitcast(FP8X4),
                        rhs_scale=x_plane[:, first : first + HALF],
                        start=(which == 0 and t == 0),
                        stop=(which == 1 and t == PACK - 1),
                    )

        w1_mx = quantize("w1", "w1_codes", round_weight("w1_grouped", w1_raw, W1_SCALAR_GROUPS), 1)
        w2_mx = quantize("w2", "w2_codes", round_weight("w2_grouped", w2_raw, W2_SCALAR_GROUPS), PACK)
        project(0, x_first)
        project(1, pick_columns(1, "w2_raw"))

        row_values = keep.tile([P, 2 * THRESHOLD_COLUMN], F32, tag="w1_raw", align_bytes=64)
        slope = row_values[:, 0:BLOCKS]
        threshold = row_values[:, THRESHOLD_COLUMN : THRESHOLD_COLUMN + BLOCKS]
        with nc.allow_non_contiguous_dma(reason="one value a partition and row block"):
            nc.sync.dma_start(slope, sl.rearrange("(u p) o -> p (u o)", p=P))
            nc.sync.dma_start(threshold, th.rearrange("(u p) o -> p (u o)", p=P))
        slope_times_threshold = keep.tile([P, BLOCKS], F32)
        nc.gpsimd.tensor_tensor(slope_times_threshold[:], slope, threshold, ALU.mult)
        bias = keep.tile([P, BLOCKS], F32)
        nc.gpsimd.tensor_scalar(bias[:], slope_times_threshold[:], -1.0, 0.0, ALU.mult, ALU.add)

        def weigh(half):
            z = keep.tile([P, HALF * PACK], BF16, name="z%d" % half, tag="z", align_bytes=64)
            nc.vector.tensor_tensor(
                z[:].rearrange("p (c i t) -> p c t i", i=PACK, t=PACK),
                y_banks[half][:].rearrange("p t (c i) -> p c t i", i=PACK),
                gain[:].unsqueeze(1).unsqueeze(3).to_broadcast([P, HALF // PACK, PACK, PACK]),
                ALU.mult,
            )
            return z

        def pick_codewords(pair, tag):
            picked = keep.tile([P, 2 * P], U32, name="d%d" % pair, tag=tag, align_bytes=64)
            nc.vector.tensor_copy(picked[:], d_table[:].bitcast(U32).indirect(entries(k1_list, pair * 2 * P, 2 * P)))
            return picked

        h = [keep.tile([P, 2, S], F32, name="h%d" % pair) for pair in range(2)]
        ds = [keep.tile([P, WINDOW], F32, name="ds%d" % u) for u in range(BLOCKS)]
        codewords = []
        z_mx = []

        def multiply(target, u, half):
            codes, scales = z_mx[half]
            nc.tensor.matmul_mx(
                out=target,
                lhsT=codewords[u // 2][:, (u % 2) * P : (u % 2 + 1) * P].bitcast(FP8X4),
                lhsT_scale=d_plane[:, u * P : (u + 1) * P],
                rhs=codes[:].bitcast(FP8X4),
                rhs_scale=scales[:],
                start=True,
                stop=True,
            )

        def first_products():
            for u in range(2):
                bank = h_psum.tile([P, HALF], F32, name="h_first", tag="h_bank")
                multiply(bank[:], u, 0)
                nc.scalar.activation(out=h[0][:, u, 0:HALF], in_=bank[:], func=ACT.Copy, scale=H_SCALE)

        def pair_products(pair, half):
            bank = h_psum.tile([P, 2, HALF], F32, name="h_pair", tag="h_bank")
            for member in range(2):
                multiply(bank[:, member, :], 2 * pair + member, half)
            nc.vector.tensor_scalar(h[pair][:, :, half * HALF : (half + 1) * HALF], bank[:], H_SCALE, None, ALU.mult)

        def send(u, half):
            nc.scalar.activation(
                out=ds[u][:].indirect(entries(n1_list, half * HALF, HALF)),
                in_=h[u // 2][:, u % 2, half * HALF : (half + 1) * HALF],
                func=ACT.Copy,
            )

        def fetch(u, first, count):
            places = slice(first, first + count)
            sg = keep.tile([P, count], F32, name="sg%d_%d" % (u, first))
            nc.scalar.activation(
                out=sg[:],
                in_=ds[u][:].indirect(entries(n2_list, first, count)),
                func=ACT.Sigmoid,
                scale=slope[:, u : u + 1],
                bias=bias[:, u : u + 1],
            )
            result = keep.tile([P, count], F32, name="result%d_%d" % (u, first))
            nc.vector.tensor_tensor(result[:], h[u // 2][:, u % 2, places], sg[:], ALU.mult)
            nc.sync.dma_start(out[u * P : (u + 1) * P, places], result[:])

        z_first = weigh(0)
        codewords.append(pick_codewords(0, "d0"))
        z_mx.append(quantize("z0", "d_bytes", z_first, 1))
        z_second = weigh(1)
        first_products()
        z_mx.append(quantize("z1", "z1_codes", z_second, 1))
        pair_products(0, 1)
        codewords.append(pick_codewords(1, "z"))
        pair_products(1, 0)
        pair_products(1, 1)

        for pair in range(2):
            members = (2 * pair, 2 * pair + 1)
            for half in range(2):
                for u in members:
                    send(u, half)
            for u in members:
                width = HALF if u == BLOCKS - 1 else S
                for first in range(0, S, width):
                    fetch(u, first, width)
